import numpy as np
import ml_dtypes


def mxq(x, axis, fmt="e4m3"):
    dtype, down = {"e4m3": (ml_dtypes.float8_e4m3fn, 7), "e5m2": (ml_dtypes.float8_e5m2, 14)}[fmt]
    v = np.moveaxis(np.asarray(x, np.float32).astype(ml_dtypes.bfloat16).astype(np.float64), axis, -1)
    blocks = v.reshape(v.shape[:-1] + (-1, 32))
    amax = np.abs(blocks).max(-1, keepdims=True)
    byte = np.maximum(np.where(amax > 0, np.frexp(amax)[1] - 1 + 127, 0) - down, 1)
    scale = np.exp2(byte - 127.0)
    codes = (blocks / scale).astype(np.float32).astype(dtype).astype(np.float64)
    return np.moveaxis((codes * scale).reshape(v.shape), -1, axis)


WIDE = False


def mx_kscale(k):
    if not WIDE:
        return np.ones(k)
    levels = np.array([30, -30])
    if k % 512:
        return np.exp2(np.random.permutation(np.resize(levels, k // 32))).repeat(32)
    a = np.empty((k // 512, 16))
    for p in range(k // 512):
        a[p, :8] = np.random.permutation(np.resize(levels, 8))
        for g in range(8):
            far = levels[np.abs(levels - a[p, g]) >= 10]
            a[p, g + 8] = far[np.random.randint(len(far))]
    return np.exp2(a.ravel()).repeat(32)


def f64(x):
    return np.asarray(x).astype(np.float64)


def striped(idx):
    return np.tile(np.asarray(idx).reshape(-1, 16).T, (8, 1)).astype(np.uint16)


def unstriped(offs):
    return offs[:16].T.reshape(-1).astype(np.int64)


E2M1 = np.array([0.0, 0.5, 1.0, 1.5, 2.0, 3.0, 4.0, 6.0, -0.0, -0.5, -1.0, -1.5, -2.0, -3.0, -4.0, -6.0])


def pack_weight(w, fmt):
    k, n = w.shape
    w = f64(np.asarray(w, np.float32).astype(ml_dtypes.bfloat16)).reshape(k // 32, 32, n)
    amax = np.abs(w).max(1)
    if fmt in ("e4m3", "e5m2"):
        byte = np.frexp(amax)[1] - 1 + 127 - (7 if fmt == "e4m3" else 14)
    else:
        mant, ex = np.frexp(amax / 6.0)
        byte = np.where(mant > 0.5, ex, ex - 1) + 127
    byte = np.clip(np.where(amax > 0, byte, 1), 1, 254)
    scaled = (w * np.exp2(127.0 - byte)[:, None, :]).reshape(k, n).astype(np.float32)
    by_word = np.ascontiguousarray(scaled.reshape(k // 512, 128, 4, n).transpose(0, 1, 3, 2))
    if fmt in ("e4m3", "e5m2"):
        words = by_word.astype(ml_dtypes.float8_e4m3fn if fmt == "e4m3" else ml_dtypes.float8_e5m2).view(np.uint8)
    else:
        c = by_word.astype(ml_dtypes.float4_e2m1fn).view(np.uint8) & 0xF
        words = (c[..., 0::2] | (c[..., 1::2] << 4)).reshape(k // 512, 128, 2 * n)
    return np.ascontiguousarray(words), np.ascontiguousarray(byte.astype(np.uint8).reshape(k // 512, 16, n))


def unpack_weight(words, scales, fmt):
    g, _, n = scales.shape
    words = np.ascontiguousarray(words).reshape(g, 128, n, -1)
    if fmt in ("e4m3", "e5m2"):
        vals = words.view(ml_dtypes.float8_e4m3fn if fmt == "e4m3" else ml_dtypes.float8_e5m2).astype(np.float64)
    else:
        nib = np.empty((g, 128, n, 4), np.uint8)
        nib[..., 0::2] = words & 0xF
        nib[..., 1::2] = words >> 4
        vals = E2M1[nib]
    vals = vals * np.repeat(np.exp2(scales.astype(np.float64) - 127.0), 8, axis=1)[..., None]
    return vals.transpose(0, 1, 3, 2).reshape(g * 512, n)


K, T, J, R, O, N, E = 512, 1024, 256, 512, 128, 256, 1024


def setup_inputs():
    n = np.random.standard_normal
    idx = np.random.permutation(T)[:J]
    idx2 = np.random.permutation(J)[:O]
    idx3 = np.random.permutation(J)[:O]
    idx4 = np.random.permutation(E)[:O]
    fk = mx_kscale(K)
    fr = mx_kscale(R)
    xtp = pack_weight(n((K, T)) / fk[:, None], "e2m1")
    wp = pack_weight(n((K, R)) * 1 / np.sqrt(K) * fk[:, None], "e5m2")
    w2p = pack_weight(n((K, R)) * 1 / np.sqrt(K) * fk[:, None], "e4m3")
    wbp = pack_weight(n((R, N)) * 1 / np.sqrt(R) / fr[:, None], "e4m3")
    return {
        "xt_words": xtp[0],
        "xt_scales": xtp[1],
        "w_words": wp[0],
        "w_scales": wp[1],
        "w2_words": w2p[0],
        "w2_scales": w2p[1],
        "sl": (np.random.uniform(1.0, 6.0, (R, 1)) * fr[:, None]).astype(np.float32),
        "sm": (np.random.uniform(1.0, 6.0, (R, 1)) * fr[:, None]).astype(np.float32),
        "wb_words": wbp[0],
        "wb_scales": wbp[1],
        "tz": (np.random.randint(-9, 10, (N, E)).astype(np.float64)).astype(np.float32),
        "so": (np.random.uniform(0.1, 0.3, (N, 1))).astype(np.float32),
        "offs": striped(idx),
        "offs2": striped(idx2),
        "offs3": striped(idx3),
        "offs4": striped(idx4),
    }


def reference(xt_words, xt_scales, w_words, w_scales, w2_words, w2_scales, sl, sm, wb_words, wb_scales, tz, so, offs, offs2, offs3, offs4):
    idx = unstriped(offs)
    idx2 = unstriped(offs2)
    idx3 = unstriped(offs3)
    idx4 = unstriped(offs4)
    xtu = unpack_weight(xt_words, xt_scales, "e2m1")
    wu = unpack_weight(w_words, w_scales, "e5m2")
    w2u = unpack_weight(w2_words, w2_scales, "e4m3")
    wbu = unpack_weight(wb_words, wb_scales, "e4m3")
    xtidxg = xtu[:, idx]
    a = wu.T @ xtidxg
    b = w2u.T @ xtidxg
    lu = f64(sl) / (1.0 + np.max(b, axis=1, keepdims=True))
    lv = f64(sm) / (1.0 + np.max(a, axis=1, keepdims=True))
    hid = np.abs(a[:, idx2] * lu - b[:, idx3] * lv)
    hidq = mxq(hid, 0, "e5m2")
    p = wbu.T @ hidq
    y = np.maximum(p, f64(tz)[:, idx4] * f64(so))
    return y

@@ -1,0 +1,189 @@
+from contextlib import ExitStack
+
+import concourse.mybir as mybir
+
+K, T, J, R, O, N, E = 512, 1024, 256, 512, 128, 256, 1024
+FLOPS = 2 * (2 * K * R * J + R * N * O)
+
+F32 = mybir.dt.float32
+BF16 = mybir.dt.bfloat16
+I32 = mybir.dt.int32
+U32 = mybir.dt.uint32
+U16 = mybir.dt.uint16
+U8 = mybir.dt.uint8
+E2M1 = mybir.dt.float4_e2m1fn_x4
+E4M3 = mybir.dt.float8_e4m3fn_x4
+E5M2 = mybir.dt.float8_e5m2_x4
+ALU = mybir.AluOpType
+ACT = mybir.ActivationFunctionType
+
+P = 128
+PACK = 4
+QUADS = 4
+
+
+def load_scale_rows(queues, plane, scales):
+    for q in range(QUADS):
+        queues[q].dma_start(
+            out=plane[32 * q : 32 * q + 4, :].bitcast(I32),
+            in_=scales[0, 4 * q : 4 * q + 4, :].bitcast(I32),
+        )
+
+
+def tile_list_loudness_twow_one_stepfloor_kernel(
+    tc, xt_words, xt_scales, w_words, w_scales, w2_words, w2_scales, sl, sm,
+    wb_words, wb_scales, tz, so, offs, offs2, offs3, offs4, out,
+):
+    nc = tc.nc
+    with ExitStack() as ctx:
+        lists = ctx.enter_context(tc.tile_pool(name="lists", bufs=1))
+        sb = ctx.enter_context(tc.tile_pool(name="sb", bufs=1))
+        ps = ctx.enter_context(tc.psum_pool(name="ps", bufs=1))
+
+        idx = lists.tile([P, J // 16], U16, name="idx")
+        idx2 = lists.tile([P, O // 16], U16, name="idx2")
+        idx3 = lists.tile([P, O // 16], U16, name="idx3")
+        idx4 = lists.tile([P, O // 16], U16, name="idx4")
+
+        x_words = sb.tile([P, T], U16, name="x_words", align_bytes=64)
+        x_plane = sb.tile([P, T], U8, name="x_plane", align_bytes=64)
+        w_raw = [sb.tile([P, R], U32, name=f"w_raw{i}", align_bytes=64) for i in range(2)]
+        w_raw_plane = sb.tile([P, 2, R], U8, name="w_raw_plane", align_bytes=64)
+        wb_codes = sb.tile([P, N], U32, name="wb_codes", align_bytes=64)
+        wb_plane = sb.tile([P, N], U8, name="wb_plane", align_bytes=64)
+        tz_rows = [sb.tile([P, E], F32, name=f"tz_rows{h}") for h in range(2)]
+        level = [sb.tile([P, PACK], F32, name=f"level{i}") for i in range(2)]
+        step = sb.tile([P, 2], F32, name="step")
+
+        nc.vector.memset(x_plane[:].bitcast(I32), 0)
+        nc.vector.memset(w_raw_plane[:].bitcast(I32), 0)
+        nc.vector.memset(wb_plane[:].bitcast(I32), 0)
+
+        words_in = [w2_words, w_words]
+        scales_in = [w2_scales, w_scales]
+        fmt = [E4M3, E5M2]
+        sync4 = [nc.sync] * QUADS
+
+        def load_words(tile, words):
+            nc.sync.dma_start(out=tile[:].bitcast(I32), in_=words[0].rearrange("p n t -> p (n t)").bitcast(I32))
+
+        nc.sync.dma_start(idx[:], offs)
+        nc.sync.dma_start(out=x_words[:].bitcast(I32), in_=xt_words[0].bitcast(I32))
+        load_words(w_raw[0], words_in[0])
+        load_scale_rows(sync4, x_plane, xt_scales)
+        load_words(w_raw[1], words_in[1])
+        load_scale_rows(sync4, w_raw_plane[:, 0, :], scales_in[0])
+        load_scale_rows(sync4, w_raw_plane[:, 1, :], scales_in[1])
+        nc.sync.dma_start(out=level[0][:], in_=sl.rearrange("(p t) o -> p (t o)", t=PACK))
+        nc.sync.dma_start(out=level[1][:], in_=sm.rearrange("(p t) o -> p (t o)", t=PACK))
+        nc.sync.dma_start(idx2[:], offs2)
+        nc.sync.dma_start(idx3[:], offs3)
+        nc.sync.dma_start(idx4[:], offs4)
+        for h in range(2):
+            nc.sync.dma_start(out=tz_rows[h][:], in_=tz[h * P : (h + 1) * P, :])
+        load_words(wb_codes, wb_words)
+        load_scale_rows(sync4, wb_plane, wb_scales)
+        with nc.allow_non_contiguous_dma(reason="one step a partition"):
+            nc.sync.dma_start(out=step[:], in_=so.rearrange("(h p) o -> p (h o)", p=P))
+
+        xg_words = sb.tile([P, J], U16, name="xg_words", align_bytes=64)
+        xg_plane = sb.tile([P, J], U8, name="xg_plane", align_bytes=64)
+        nc.vector.tensor_copy(xg_words[:], x_words[:].indirect(idx[:]))
+        nc.vector.tensor_copy(xg_plane[:], x_plane[:].indirect(idx[:]))
+
+        w_codes = [sb.tile([P, PACK, P], U32, name=f"w_codes{i}", align_bytes=64) for i in range(2)]
+        w_plane = sb.tile([P, 2, PACK, P], U8, name="w_plane", align_bytes=64)
+        for i in range(2):
+            nc.scalar.copy(
+                out=w_codes[i][:].rearrange("p t (c m) -> p c t m", m=4),
+                in_=w_raw[i][:].rearrange("p (c m t) -> p c t m", m=4, t=PACK),
+            )
+        for u in range(2):
+            ts = slice(2 * u, 2 * u + 2)
+            nc.vector.tensor_copy(
+                out=w_plane[:].rearrange("p i t (c m) -> p i c t m", m=16)[:, :, :, ts, :],
+                in_=w_raw_plane[:].rearrange("p i (c m t) -> p i c t m", m=16, t=PACK)[:, :, :, ts, :],
+            )
+
+        inv_level = sb.tile([P, 2 * PACK], F32, name="inv_level")
+        for i in range(2):
+            nc.vector.reciprocal(inv_level[:, i :: 2], level[i][:])
+
+        top = sb.tile([P, 2 * PACK], F32, name="top")
+        inv_gain = sb.tile([P, 2 * PACK], F32, name="inv_gain")
+        gain = sb.tile([P, 2 * PACK], F32, name="gain")
+        picked = [sb.tile([P, PACK, O], F32, name=f"picked{i}") for i in range(2)]
+        side_idx = [idx3, idx2]
+
+        rows = {}
+
+        def pick(i, t):
+            nc.scalar.activation(
+                out=picked[i][:, t, :], in_=rows[2 * t + i][:].indirect(side_idx[i][:]), func=ACT.Copy,
+                scale=gain[:, 2 * t + 1 - i : 2 * t + 2 - i],
+            )
+
+        for t in range(PACK):
+            for i in range(2):
+                c = 2 * t + i
+                acc = ps.tile([P, J], F32, name=f"acc{i}{t}")
+                nc.tensor.matmul_mx(
+                    out=acc[:], lhsT=w_codes[i][:, t, :].bitcast(fmt[i]), lhsT_scale=w_plane[:, i, t, :],
+                    rhs=xg_words[:].bitcast(E2M1), rhs_scale=xg_plane[:], start=True, stop=True,
+                )
+                row = sb.tile([P, J], F32, name=f"rows{i}{t}")
+                nc.vector.tensor_scalar(
+                    out=row[:], in0=acc[:], scalar1=0.0, scalar2=None, op0=ALU.add, op1=ALU.max,
+                    accum_out=top[:, c : c + 1],
+                )
+                rows[c] = row
+                last = c == 2 * PACK - 1
+                (nc.vector if last else nc.gpsimd).tensor_scalar(
+                    out=inv_gain[:, c : c + 1], in0=top[:, c : c + 1], scalar1=1.0,
+                    scalar2=inv_level[:, c : c + 1], op0=ALU.add, op1=ALU.mult,
+                )
+                if i == 0 or last:
+                    cs = slice(c if last else max(c - 1, 0), c + 1)
+                    nc.vector.reciprocal(gain[:, cs], inv_gain[:, cs])
+                if i == 0 and t > 0:
+                    pick(0, t - 1)
+                if i == 1:
+                    pick(1, t)
+        pick(0, PACK - 1)
+
+        diff = sb.tile([P, PACK, O], F32, name="diff", tag="diff")
+        for t in range(PACK):
+            nc.vector.tensor_tensor(diff[:, t, :], picked[1][:, t, :], picked[0][:, t, :], ALU.subtract)
+
+        hid = sb.tile([P, O, PACK], BF16, name="hid", align_bytes=64)
+        half = O // 2
+        woven = diff[:].rearrange("p t o -> p o t")
+        nc.vector.scalar_tensor_tensor(
+            out=hid[:, :half, :], in0=woven[:, :half, :], scalar=-1.0, in1=woven[:, :half, :],
+            op0=ALU.mult, op1=ALU.max,
+        )
+        nc.scalar.activation(out=hid[:, half:, :], in_=woven[:, half:, :], func=ACT.Abs)
+
+        hid_codes = sb.tile([P, O], U32, name="hid_codes", align_bytes=64)
+        hid_plane = sb.tile([P, O], U8, name="hid_plane", align_bytes=64)
+        nc.vector.quantize_mx(
+            out=hid_codes[:].bitcast(E5M2), scales=hid_plane[:], in_=hid[:].rearrange("p o t -> p (o t)")
+        )
+
+        floor = sb.tile([P, 2, O], F32, name="floor", tag="diff")
+        for h in range(2):
+            nc.scalar.activation(
+                out=floor[:, h, :], in_=tz_rows[h][:].indirect(idx4[:]), func=ACT.Copy, scale=step[:, h : h + 1]
+            )
+
+        queues = [nc.sync, nc.scalar]
+        for h in range(2):
+            cols = slice(h * P, (h + 1) * P)
+            prod = ps.tile([P, O], F32, name=f"prod{h}", tag=f"acc{h}0")
+            nc.tensor.matmul_mx(
+                out=prod[:], lhsT=wb_codes[:, cols].bitcast(E4M3), lhsT_scale=wb_plane[:, cols],
+                rhs=hid_codes[:].bitcast(E5M2), rhs_scale=hid_plane[:], start=True, stop=True,
+            )
+            res = sb.tile([P, O], F32, name=f"res{h}")
+            nc.vector.tensor_tensor(res[:], prod[:], floor[:, h, :], ALU.max)
+            queues[h].dma_start(out=out[cols, :], in_=res[:])

@@ -64,27 +64,27 @@ def tile_list_loudness_twow_one_stepfloor_kernel(
         fmt = [E4M3, E5M2]
         sync4 = [nc.sync] * QUADS
 
-        def load_words(tile, words):
-            nc.sync.dma_start(out=tile[:].bitcast(I32), in_=words[0].rearrange("p n t -> p (n t)").bitcast(I32))
+        def load_words(queue, tile, words):
+            queue.dma_start(out=tile[:].bitcast(I32), in_=words[0].rearrange("p n t -> p (n t)").bitcast(I32))
 
         nc.sync.dma_start(idx[:], offs)
-        nc.sync.dma_start(out=x_words[:].bitcast(I32), in_=xt_words[0].bitcast(I32))
-        load_words(w_raw[0], words_in[0])
-        load_scale_rows(sync4, x_plane, xt_scales)
-        load_words(w_raw[1], words_in[1])
-        load_scale_rows(sync4, w_raw_plane[:, 0, :], scales_in[0])
-        load_scale_rows(sync4, w_raw_plane[:, 1, :], scales_in[1])
         nc.sync.dma_start(out=level[0][:], in_=sl.rearrange("(p t) o -> p (t o)", t=PACK))
         nc.sync.dma_start(out=level[1][:], in_=sm.rearrange("(p t) o -> p (t o)", t=PACK))
+        nc.sync.dma_start(out=x_words[:].bitcast(I32), in_=xt_words[0].bitcast(I32))
+        load_scale_rows(sync4, x_plane, xt_scales)
+        for i in range(2):
+            load_words(nc.gpsimd, w_raw[i], words_in[i])
+        for i in range(2):
+            load_scale_rows(sync4, w_raw_plane[:, i, :], scales_in[i])
         nc.sync.dma_start(idx2[:], offs2)
         nc.sync.dma_start(idx3[:], offs3)
         nc.sync.dma_start(idx4[:], offs4)
-        for h in range(2):
-            nc.sync.dma_start(out=tz_rows[h][:], in_=tz[h * P : (h + 1) * P, :])
-        load_words(wb_codes, wb_words)
-        load_scale_rows(sync4, wb_plane, wb_scales)
         with nc.allow_non_contiguous_dma(reason="one step a partition"):
             nc.sync.dma_start(out=step[:], in_=so.rearrange("(h p) o -> p (h o)", p=P))
+        load_scale_rows(sync4, wb_plane, wb_scales)
+        for h in range(2):
+            nc.sync.dma_start(out=tz_rows[h][:], in_=tz[h * P : (h + 1) * P, :])
+        load_words(nc.sync, wb_codes, wb_words)
 
         xg_words = sb.tile([P, J], U16, name="xg_words", align_bytes=64)
         xg_plane = sb.tile([P, J], U8, name="xg_plane", align_bytes=64)
@@ -110,7 +110,7 @@ def tile_list_loudness_twow_one_stepfloor_kernel(
             nc.vector.reciprocal(inv_level[:, i :: 2], level[i][:])
 
         top = sb.tile([P, 2 * PACK], F32, name="top")
-        inv_gain = sb.tile([P, 2 * PACK], F32, name="inv_gain")
+        inv_gain = sb.tile([P, 2 * PACK], F32, name="inv_gain", tag="diff")
         gain = sb.tile([P, 2 * PACK], F32, name="gain")
         picked = [sb.tile([P, PACK, O], F32, name=f"picked{i}") for i in range(2)]
         side_idx = [idx3, idx2]
@@ -152,8 +152,8 @@ def tile_list_loudness_twow_one_stepfloor_kernel(
         pick(0, PACK - 1)
 
         diff = sb.tile([P, PACK, O], F32, name="diff", tag="diff")
-        for t in range(PACK):
-            nc.vector.tensor_tensor(diff[:, t, :], picked[1][:, t, :], picked[0][:, t, :], ALU.subtract)
+        for ts in (slice(0, PACK - 1), slice(PACK - 1, PACK)):
+            nc.vector.tensor_tensor(diff[:, ts, :], picked[1][:, ts, :], picked[0][:, ts, :], ALU.subtract)
 
         hid = sb.tile([P, O, PACK], BF16, name="hid", align_bytes=64)
         half = O // 2
@@ -170,10 +170,13 @@ def tile_list_loudness_twow_one_stepfloor_kernel(
             out=hid_codes[:].bitcast(E5M2), scales=hid_plane[:], in_=hid[:].rearrange("p o t -> p (o t)")
         )
 
-        floor = sb.tile([P, 2, O], F32, name="floor", tag="diff")
+        floor = [
+            sb.tile([P, O], F32, name="floor0", tag="rows03"),
+            sb.tile([P, O], F32, name="floor1", tag="diff"),
+        ]
         for h in range(2):
             nc.scalar.activation(
-                out=floor[:, h, :], in_=tz_rows[h][:].indirect(idx4[:]), func=ACT.Copy, scale=step[:, h : h + 1]
+                out=floor[h][:], in_=tz_rows[h][:].indirect(idx4[:]), func=ACT.Copy, scale=step[:, h : h + 1]
             )
 
         queues = [nc.sync, nc.scalar]
@@ -185,5 +188,5 @@ def tile_list_loudness_twow_one_stepfloor_kernel(
                 rhs=hid_codes[:].bitcast(E5M2), rhs_scale=hid_plane[:], start=True, stop=True,
             )
             res = sb.tile([P, O], F32, name=f"res{h}")
-            nc.vector.tensor_tensor(res[:], prod[:], floor[:, h, :], ALU.max)
+            nc.vector.tensor_tensor(res[:], prod[:], floor[h][:], ALU.max)
             queues[h].dma_start(out=out[cols, :], in_=res[:])

from contextlib import ExitStack

import concourse.mybir as mybir

K, T, J, R, O, N, E = 512, 1024, 256, 512, 128, 256, 1024
FLOPS = 2 * (2 * K * R * J + R * N * O)

F32 = mybir.dt.float32
BF16 = mybir.dt.bfloat16
I32 = mybir.dt.int32
U32 = mybir.dt.uint32
U16 = mybir.dt.uint16
U8 = mybir.dt.uint8
E2M1 = mybir.dt.float4_e2m1fn_x4
E4M3 = mybir.dt.float8_e4m3fn_x4
E5M2 = mybir.dt.float8_e5m2_x4
ALU = mybir.AluOpType
ACT = mybir.ActivationFunctionType

P = 128
PACK = 4
QUADS = 4


def load_scale_rows(queues, plane, scales):
    for q in range(QUADS):
        queues[q].dma_start(
            out=plane[32 * q : 32 * q + 4, :].bitcast(I32),
            in_=scales[0, 4 * q : 4 * q + 4, :].bitcast(I32),
        )


def tile_list_loudness_twow_one_stepfloor_kernel(
    tc, xt_words, xt_scales, w_words, w_scales, w2_words, w2_scales, sl, sm,
    wb_words, wb_scales, tz, so, offs, offs2, offs3, offs4, out,
):
    nc = tc.nc
    with ExitStack() as ctx:
        lists = ctx.enter_context(tc.tile_pool(name="lists", bufs=1))
        sb = ctx.enter_context(tc.tile_pool(name="sb", bufs=1))
        ps = ctx.enter_context(tc.psum_pool(name="ps", bufs=1))

        idx = lists.tile([P, J // 16], U16, name="idx")
        idx2 = lists.tile([P, O // 16], U16, name="idx2")
        idx3 = lists.tile([P, O // 16], U16, name="idx3")
        idx4 = lists.tile([P, O // 16], U16, name="idx4")

        x_words = sb.tile([P, T], U16, name="x_words", align_bytes=64)
        x_plane = sb.tile([P, T], U8, name="x_plane", align_bytes=64)
        w_raw = [sb.tile([P, R], U32, name=f"w_raw{i}", align_bytes=64) for i in range(2)]
        w_raw_plane = sb.tile([P, 2, R], U8, name="w_raw_plane", align_bytes=64)
        wb_codes = sb.tile([P, N], U32, name="wb_codes", align_bytes=64)
        wb_plane = sb.tile([P, N], U8, name="wb_plane", align_bytes=64)
        tz_rows = [sb.tile([P, E], F32, name=f"tz_rows{h}") for h in range(2)]
        level = [sb.tile([P, PACK], F32, name=f"level{i}") for i in range(2)]
        step = sb.tile([P, 2], F32, name="step")

        nc.vector.memset(x_plane[:].bitcast(I32), 0)
        nc.vector.memset(w_raw_plane[:].bitcast(I32), 0)
        nc.vector.memset(wb_plane[:].bitcast(I32), 0)

        words_in = [w2_words, w_words]
        scales_in = [w2_scales, w_scales]
        fmt = [E4M3, E5M2]
        sync4 = [nc.sync] * QUADS

        def load_words(queue, tile, words):
            queue.dma_start(out=tile[:].bitcast(I32), in_=words[0].rearrange("p n t -> p (n t)").bitcast(I32))

        nc.sync.dma_start(idx[:], offs)
        nc.sync.dma_start(out=level[0][:], in_=sl.rearrange("(p t) o -> p (t o)", t=PACK))
        nc.sync.dma_start(out=level[1][:], in_=sm.rearrange("(p t) o -> p (t o)", t=PACK))
        nc.sync.dma_start(out=x_words[:].bitcast(I32), in_=xt_words[0].bitcast(I32))
        load_scale_rows(sync4, x_plane, xt_scales)
        for i in range(2):
            load_words(nc.gpsimd, w_raw[i], words_in[i])
        for i in range(2):
            load_scale_rows(sync4, w_raw_plane[:, i, :], scales_in[i])
        nc.sync.dma_start(idx2[:], offs2)
        nc.sync.dma_start(idx3[:], offs3)
        nc.sync.dma_start(idx4[:], offs4)
        with nc.allow_non_contiguous_dma(reason="one step a partition"):
            nc.sync.dma_start(out=step[:], in_=so.rearrange("(h p) o -> p (h o)", p=P))
        load_scale_rows(sync4, wb_plane, wb_scales)
        for h in range(2):
            nc.sync.dma_start(out=tz_rows[h][:], in_=tz[h * P : (h + 1) * P, :])
        load_words(nc.sync, wb_codes, wb_words)

        xg_words = sb.tile([P, J], U16, name="xg_words", align_bytes=64)
        xg_plane = sb.tile([P, J], U8, name="xg_plane", align_bytes=64)
        nc.vector.tensor_copy(xg_words[:], x_words[:].indirect(idx[:]))
        nc.vector.tensor_copy(xg_plane[:], x_plane[:].indirect(idx[:]))

        w_codes = [sb.tile([P, PACK, P], U32, name=f"w_codes{i}", align_bytes=64) for i in range(2)]
        w_plane = sb.tile([P, 2, PACK, P], U8, name="w_plane", align_bytes=64)
        for i in range(2):
            nc.scalar.copy(
                out=w_codes[i][:].rearrange("p t (c m) -> p c t m", m=4),
                in_=w_raw[i][:].rearrange("p (c m t) -> p c t m", m=4, t=PACK),
            )
        for u in range(2):
            ts = slice(2 * u, 2 * u + 2)
            nc.vector.tensor_copy(
                out=w_plane[:].rearrange("p i t (c m) -> p i c t m", m=16)[:, :, :, ts, :],
                in_=w_raw_plane[:].rearrange("p i (c m t) -> p i c t m", m=16, t=PACK)[:, :, :, ts, :],
            )

        inv_level = sb.tile([P, 2 * PACK], F32, name="inv_level")
        for i in range(2):
            nc.vector.reciprocal(inv_level[:, i :: 2], level[i][:])

        top = sb.tile([P, 2 * PACK], F32, name="top")
        inv_gain = sb.tile([P, 2 * PACK], F32, name="inv_gain", tag="diff")
        gain = sb.tile([P, 2 * PACK], F32, name="gain")
        picked = [sb.tile([P, PACK, O], F32, name=f"picked{i}") for i in range(2)]
        side_idx = [idx3, idx2]

        rows = {}

        def pick(i, t):
            nc.scalar.activation(
                out=picked[i][:, t, :], in_=rows[2 * t + i][:].indirect(side_idx[i][:]), func=ACT.Copy,
                scale=gain[:, 2 * t + 1 - i : 2 * t + 2 - i],
            )

        for t in range(PACK):
            for i in range(2):
                c = 2 * t + i
                acc = ps.tile([P, J], F32, name=f"acc{i}{t}")
                nc.tensor.matmul_mx(
                    out=acc[:], lhsT=w_codes[i][:, t, :].bitcast(fmt[i]), lhsT_scale=w_plane[:, i, t, :],
                    rhs=xg_words[:].bitcast(E2M1), rhs_scale=xg_plane[:], start=True, stop=True,
                )
                row = sb.tile([P, J], F32, name=f"rows{i}{t}")
                nc.vector.tensor_scalar(
                    out=row[:], in0=acc[:], scalar1=0.0, scalar2=None, op0=ALU.add, op1=ALU.max,
                    accum_out=top[:, c : c + 1],
                )
                rows[c] = row
                last = c == 2 * PACK - 1
                (nc.vector if last else nc.gpsimd).tensor_scalar(
                    out=inv_gain[:, c : c + 1], in0=top[:, c : c + 1], scalar1=1.0,
                    scalar2=inv_level[:, c : c + 1], op0=ALU.add, op1=ALU.mult,
                )
                if i == 0 or last:
                    cs = slice(c if last else max(c - 1, 0), c + 1)
                    nc.vector.reciprocal(gain[:, cs], inv_gain[:, cs])
                if i == 0 and t > 0:
                    pick(0, t - 1)
                if i == 1:
                    pick(1, t)
        pick(0, PACK - 1)

        diff = sb.tile([P, PACK, O], F32, name="diff", tag="diff")
        for ts in (slice(0, PACK - 1), slice(PACK - 1, PACK)):
            nc.vector.tensor_tensor(diff[:, ts, :], picked[1][:, ts, :], picked[0][:, ts, :], ALU.subtract)

        hid = sb.tile([P, O, PACK], BF16, name="hid", align_bytes=64)
        half = O // 2
        woven = diff[:].rearrange("p t o -> p o t")
        nc.vector.scalar_tensor_tensor(
            out=hid[:, :half, :], in0=woven[:, :half, :], scalar=-1.0, in1=woven[:, :half, :],
            op0=ALU.mult, op1=ALU.max,
        )
        nc.scalar.activation(out=hid[:, half:, :], in_=woven[:, half:, :], func=ACT.Abs)

        hid_codes = sb.tile([P, O], U32, name="hid_codes", align_bytes=64)
        hid_plane = sb.tile([P, O], U8, name="hid_plane", align_bytes=64)
        nc.vector.quantize_mx(
            out=hid_codes[:].bitcast(E5M2), scales=hid_plane[:], in_=hid[:].rearrange("p o t -> p (o t)")
        )

        floor = [
            sb.tile([P, O], F32, name="floor0", tag="rows03"),
            sb.tile([P, O], F32, name="floor1", tag="diff"),
        ]
        for h in range(2):
            nc.scalar.activation(
                out=floor[h][:], in_=tz_rows[h][:].indirect(idx4[:]), func=ACT.Copy, scale=step[:, h : h + 1]
            )

        queues = [nc.sync, nc.scalar]
        for h in range(2):
            cols = slice(h * P, (h + 1) * P)
            prod = ps.tile([P, O], F32, name=f"prod{h}", tag=f"acc{h}0")
            nc.tensor.matmul_mx(
                out=prod[:], lhsT=wb_codes[:, cols].bitcast(E4M3), lhsT_scale=wb_plane[:, cols],
                rhs=hid_codes[:].bitcast(E5M2), rhs_scale=hid_plane[:], start=True, stop=True,
            )
            res = sb.tile([P, O], F32, name=f"res{h}")
            nc.vector.tensor_tensor(res[:], prod[:], floor[h][:], ALU.max)
            queues[h].dma_start(out=out[cols, :], in_=res[:])
